import numpy as np, ml_dtypes
CORES = [115,116,123,124]
N = 4
TOK = 512
ROUTE = [[[2,3],[1,2],[1,2],[2,3],[1,2],[1,2],[2,3],[0,2],[0,1],[1,2],[0,2],[1,2],[0,2],[1,2],[1,2],[2,3],[0,3],[1,2],[1,2],[1,2],[1,2],[0,2],[0,2],[1,2],[2,3],[0,2],[1,2],[0,2],[2,3],[2,3],[0,2],[2,3],[2,3],[1,2],[1,2],[0,2],[2,3],[1,2],[1,2],[0,2],[0,2],[1,2],[2,3],[1,2],[0,2],[0,2],[0,1],[0,2],[0,2],[1,2],[0,2],[0,2],[1,3],[1,2],[2,3],[2,3],[0,2],[2,3],[2,3],[0,2],[2,3],[0,2],[0,2],[1,2],[0,3],[0,3],[2,3],[2,3],[1,2],[0,1],[1,3],[2,3],[1,3],[0,2],[2,3],[0,1],[1,2],[1,2],[1,2],[1,2],[0,2],[2,3],[2,3],[2,3],[0,3],[1,2],[2,3],[1,2],[0,2],[0,2],[0,2],[1,2],[0,2],[1,2],[2,3],[2,3],[1,2],[0,1],[1,2],[0,2],[0,2],[2,3],[1,2],[1,2],[1,2],[2,3],[2,3],[0,2],[2,3],[0,2],[2,3],[1,2],[1,3],[0,2],[2,3],[1,3],[2,3],[1,2],[1,3],[1,2],[2,3],[0,2],[2,3],[0,2],[2,3],[2,3],[1,2],[2,3],[2,3],[0,2],[1,2],[2,3],[1,2],[2,3],[1,2],[1,2],[1,2],[0,1],[1,2],[2,3],[0,2],[0,2],[0,3],[1,3],[0,3],[0,2],[2,3],[1,2],[0,2],[0,3],[0,3],[0,2],[0,2],[0,3],[2,3],[1,2],[0,3],[0,3],[0,1],[0,2],[1,2],[1,3],[0,3],[0,1],[2,3],[0,2],[0,2],[0,3],[0,2],[0,1],[1,2],[1,2],[1,3],[2,3],[0,2],[0,2],[0,2],[1,2],[0,3],[0,1],[1,2],[1,2],[0,2],[1,2],[0,1],[1,2],[1,2],[2,3],[0,3],[2,3],[2,3],[1,2],[2,3],[1,2],[1,2],[2,3],[2,3],[1,2],[0,3],[2,3],[0,1],[2,3],[1,3],[1,2],[1,2],[0,2],[0,2],[1,2],[2,3],[2,3],[0,1],[2,3],[0,2],[1,3],[1,2],[0,2],[0,2],[2,3],[0,3],[0,1],[0,3],[2,3],[1,2],[0,3],[1,3],[0,2],[0,2],[0,2],[1,2],[0,2],[2,3],[2,3],[1,2],[0,2],[1,2],[1,2],[0,2],[1,2],[2,3],[2,3],[2,3],[2,3],[1,2],[2,3],[1,2],[2,3],[0,2],[1,2],[2,3],[0,2],[2,3],[1,3],[2,3],[0,2],[1,2],[1,2],[1,2],[0,2],[2,3],[0,1],[0,2],[1,2],[2,3],[0,1],[0,3],[1,2],[2,3],[0,1],[2,3],[2,3],[0,3],[2,3],[2,3],[2,3],[0,3],[1,2],[0,2],[0,2],[2,3],[0,1],[0,2],[0,2],[1,3],[0,2],[0,2],[0,2],[0,2],[1,2],[0,2],[0,1],[0,2],[1,2],[0,3],[0,1],[0,2],[0,2],[2,3],[2,3],[1,3],[2,3],[2,3],[1,2],[0,2],[2,3],[1,2],[0,1],[0,2],[0,3],[0,2],[1,2],[1,2],[2,3],[2,3],[0,2],[1,2],[0,1],[1,3],[0,1],[2,3],[1,2],[2,3],[2,3],[2,3],[2,3],[1,2],[0,2],[1,2],[0,2],[1,2],[0,2],[1,2],[0,2],[0,2],[2,3],[1,2],[1,2],[0,2],[2,3],[1,2],[2,3],[0,2],[1,2],[2,3],[1,3],[1,2],[0,3],[2,3],[1,2],[2,3],[0,2],[0,3],[0,1],[0,2],[1,2],[0,2],[0,3],[1,2],[2,3],[1,2],[0,2],[1,2],[2,3],[2,3],[2,3],[1,2],[0,2],[2,3],[1,3],[0,1],[2,3],[0,2],[0,2],[1,2],[1,2],[2,3],[1,2],[0,2],[0,1],[0,2],[2,3],[1,2],[2,3],[0,2],[0,2],[1,2],[1,2],[0,2],[2,3],[1,3],[1,2],[1,2],[2,3],[1,2],[1,2],[2,3],[2,3],[1,3],[0,2],[1,2],[1,2],[2,3],[2,3],[1,2],[1,2],[0,1],[1,2],[1,2],[2,3],[2,3],[0,1],[2,3],[1,2],[0,2],[1,2],[0,1],[1,2],[0,3],[1,2],[0,2],[0,2],[1,3],[1,3],[2,3],[0,1],[1,2],[0,1],[1,2],[1,2],[2,3],[0,3],[1,3],[1,3],[0,1],[2,3],[2,3],[2,3],[0,2],[0,2],[2,3],[1,2],[0,2],[0,2],[0,2],[1,2],[2,3],[1,2],[0,2],[0,2],[0,2],[1,2],[2,3],[1,2],[0,2],[0,1],[0,3],[2,3],[1,2],[0,2],[2,3],[1,2],[0,3],[0,1],[0,3],[0,2],[2,3],[0,2],[1,2],[0,2],[0,2],[0,3],[2,3],[1,2],[1,2],[0,2],[1,2],[0,2],[2,3],[1,2],[1,2],[1,2],[0,2],[0,2],[2,3],[2,3],[0,2],[1,2],[2,3],[0,1],[1,2],[1,2],[0,3],[2,3],[1,2],[0,2],[1,2],[1,2],[1,3],[2,3],[0,2],[0,3],[0,1],[1,2],[1,3],[1,3],[0,2],[1,2],[1,2],[2,3],[2,3],[0,2],[0,2],[0,1]],[[1,3],[0,1],[2,3],[2,3],[0,2],[2,3],[2,3],[0,2],[0,2],[1,2],[2,3],[0,1],[2,3],[2,3],[1,2],[0,3],[2,3],[0,2],[1,2],[0,3],[1,3],[0,2],[0,2],[1,2],[0,2],[1,2],[1,2],[0,2],[2,3],[2,3],[1,2],[2,3],[1,2],[2,3],[1,2],[2,3],[1,3],[0,1],[1,2],[1,2],[1,3],[0,2],[0,2],[1,2],[2,3],[0,2],[0,2],[1,2],[1,2],[0,2],[2,3],[2,3],[0,1],[1,2],[1,2],[2,3],[0,2],[2,3],[0,2],[0,2],[2,3],[1,2],[2,3],[2,3],[1,2],[2,3],[2,3],[2,3],[2,3],[2,3],[1,2],[0,1],[2,3],[0,2],[0,1],[1,3],[2,3],[1,2],[1,2],[1,3],[0,3],[0,2],[0,1],[2,3],[0,2],[1,2],[0,3],[0,3],[0,1],[2,3],[2,3],[1,2],[0,2],[1,2],[0,2],[1,2],[1,2],[0,2],[2,3],[2,3],[0,2],[0,2],[1,2],[0,3],[0,2],[2,3],[0,1],[1,2],[0,2],[1,3],[2,3],[1,2],[1,2],[1,2],[0,3],[0,2],[0,2],[0,2],[0,3],[1,2],[1,2],[2,3],[1,2],[1,2],[1,2],[0,2],[2,3],[0,1],[0,2],[2,3],[1,2],[1,2],[1,3],[2,3],[1,2],[0,2],[1,2],[0,3],[1,3],[1,2],[1,2],[0,2],[2,3],[0,1],[0,2],[0,3],[1,2],[1,2],[0,2],[1,3],[0,2],[2,3],[2,3],[2,3],[0,2],[0,2],[1,3],[2,3],[1,2],[0,3],[2,3],[2,3],[2,3],[1,2],[1,2],[0,2],[2,3],[0,2],[1,2],[0,2],[0,2],[0,3],[1,2],[2,3],[2,3],[1,3],[1,2],[0,2],[0,2],[0,2],[0,3],[1,2],[2,3],[1,3],[0,2],[1,2],[1,2],[2,3],[0,2],[1,2],[2,3],[1,3],[1,2],[0,1],[1,2],[1,2],[0,2],[0,2],[0,2],[0,2],[2,3],[0,2],[1,2],[1,2],[0,1],[2,3],[1,2],[0,2],[0,1],[1,2],[0,2],[1,3],[1,2],[2,3],[0,2],[2,3],[0,2],[1,2],[0,3],[0,1],[1,2],[0,2],[1,2],[0,2],[1,2],[2,3],[1,2],[2,3],[0,1],[0,2],[0,2],[0,2],[0,2],[0,1],[0,2],[0,2],[1,3],[1,3],[2,3],[1,2],[1,2],[0,1],[1,2],[0,3],[1,3],[0,1],[2,3],[0,2],[0,2],[1,2],[2,3],[2,3],[2,3],[2,3],[0,2],[0,2],[1,2],[0,2],[0,1],[1,2],[0,2],[0,2],[1,2],[1,2],[1,2],[0,2],[0,2],[2,3],[1,2],[0,3],[0,2],[0,2],[0,1],[0,2],[1,3],[1,2],[1,2],[1,2],[0,2],[2,3],[2,3],[1,3],[0,3],[0,2],[2,3],[2,3],[1,2],[1,2],[0,2],[1,2],[0,2],[0,2],[2,3],[2,3],[0,2],[2,3],[1,2],[0,2],[2,3],[2,3],[2,3],[2,3],[0,2],[0,2],[0,2],[0,2],[2,3],[1,2],[0,1],[1,2],[1,2],[0,2],[2,3],[1,2],[2,3],[2,3],[2,3],[0,2],[0,2],[1,2],[0,2],[0,2],[1,2],[1,3],[1,2],[0,2],[2,3],[0,1],[1,3],[0,3],[1,3],[1,2],[2,3],[2,3],[2,3],[0,2],[2,3],[0,2],[1,2],[1,2],[1,2],[0,2],[0,2],[1,2],[0,2],[2,3],[0,2],[0,2],[1,2],[1,2],[0,2],[0,2],[0,2],[0,1],[0,2],[0,2],[0,3],[0,2],[1,2],[0,3],[2,3],[2,3],[0,2],[1,2],[1,3],[1,3],[2,3],[2,3],[2,3],[0,2],[2,3],[2,3],[0,1],[2,3],[1,2],[1,2],[2,3],[1,3],[0,2],[2,3],[1,2],[0,2],[2,3],[1,2],[2,3],[2,3],[2,3],[1,3],[0,2],[2,3],[0,2],[2,3],[2,3],[2,3],[2,3],[2,3],[1,2],[0,2],[1,2],[0,1],[1,2],[2,3],[2,3],[1,2],[2,3],[0,2],[1,3],[1,3],[1,2],[1,2],[1,2],[0,2],[0,2],[2,3],[2,3],[1,2],[1,2],[1,2],[0,3],[0,2],[2,3],[0,2],[0,2],[2,3],[2,3],[0,2],[1,2],[0,2],[2,3],[1,2],[1,2],[0,2],[1,2],[2,3],[2,3],[0,1],[0,2],[2,3],[0,2],[2,3],[0,2],[0,2],[2,3],[1,2],[2,3],[0,2],[2,3],[2,3],[0,2],[1,3],[0,1],[0,2],[1,2],[0,2],[1,2],[0,2],[1,2],[1,2],[0,2],[0,2],[2,3],[0,2],[2,3],[1,2],[1,2],[2,3],[0,1],[0,2],[1,2],[0,3],[1,2],[0,2],[0,2],[0,2],[0,2],[1,2],[1,3],[1,2],[1,2],[0,2],[0,3],[2,3],[1,2],[2,3],[0,2],[2,3],[1,2],[1,2],[2,3],[0,2],[0,3],[2,3],[1,2],[1,3],[0,3],[2,3],[1,2],[0,3],[0,2],[1,2],[2,3],[2,3],[0,3],[0,2],[0,2],[1,2],[0,1],[2,3],[2,3],[1,2],[0,2],[1,2]],[[1,2],[2,3],[0,2],[1,2],[1,2],[2,3],[1,3],[1,2],[2,3],[1,2],[1,3],[0,2],[2,3],[1,2],[1,2],[1,2],[1,2],[1,2],[0,2],[2,3],[2,3],[2,3],[0,1],[0,2],[1,2],[1,2],[1,2],[0,1],[2,3],[1,2],[2,3],[0,2],[1,2],[0,2],[0,1],[1,3],[2,3],[0,1],[2,3],[1,2],[0,2],[0,2],[0,1],[0,2],[1,3],[1,2],[1,2],[1,2],[2,3],[1,2],[1,2],[0,2],[0,3],[1,2],[0,2],[0,2],[0,3],[1,2],[0,2],[1,2],[2,3],[1,3],[1,2],[0,2],[1,3],[0,1],[1,2],[2,3],[0,2],[2,3],[0,2],[1,3],[0,3],[2,3],[0,2],[2,3],[1,2],[0,2],[0,1],[1,2],[2,3],[0,2],[0,2],[2,3],[0,2],[0,3],[1,2],[2,3],[0,3],[1,2],[2,3],[0,2],[1,3],[0,2],[2,3],[2,3],[0,2],[2,3],[2,3],[0,2],[1,2],[2,3],[2,3],[2,3],[2,3],[1,3],[0,2],[2,3],[1,2],[1,2],[0,3],[0,2],[0,3],[1,2],[0,2],[0,2],[2,3],[2,3],[2,3],[2,3],[0,1],[0,2],[1,2],[2,3],[0,2],[2,3],[2,3],[2,3],[0,2],[1,2],[0,2],[1,2],[1,3],[0,2],[1,2],[0,2],[0,2],[0,2],[1,2],[0,2],[0,1],[0,2],[0,3],[0,3],[2,3],[0,1],[0,2],[1,3],[1,2],[0,2],[0,3],[0,2],[2,3],[1,2],[2,3],[1,2],[0,2],[1,2],[0,2],[0,1],[1,2],[2,3],[1,2],[1,3],[2,3],[0,1],[1,2],[0,2],[0,2],[1,2],[0,2],[1,3],[1,2],[2,3],[2,3],[1,2],[0,2],[2,3],[1,3],[0,2],[1,2],[2,3],[1,3],[1,2],[2,3],[1,2],[0,2],[2,3],[1,2],[0,2],[1,2],[1,2],[0,1],[2,3],[0,2],[0,2],[0,2],[1,2],[2,3],[2,3],[2,3],[1,3],[1,2],[0,2],[0,2],[0,2],[0,3],[0,1],[0,2],[0,2],[1,2],[1,2],[0,2],[2,3],[0,3],[2,3],[0,2],[1,2],[2,3],[1,2],[1,2],[0,3],[0,2],[1,2],[1,2],[0,3],[2,3],[2,3],[0,2],[2,3],[0,2],[0,1],[1,2],[0,3],[0,1],[1,2],[2,3],[0,3],[1,2],[1,3],[1,2],[2,3],[1,3],[0,2],[1,2],[2,3],[1,2],[1,3],[1,2],[0,3],[2,3],[2,3],[0,2],[0,2],[2,3],[2,3],[2,3],[2,3],[0,2],[2,3],[2,3],[0,2],[0,2],[0,2],[2,3],[0,2],[1,2],[1,2],[1,2],[1,2],[0,2],[0,2],[1,2],[2,3],[1,3],[0,1],[1,2],[0,1],[1,3],[0,2],[0,1],[1,2],[0,2],[1,3],[0,2],[0,2],[1,2],[0,3],[1,2],[1,2],[2,3],[1,2],[2,3],[0,1],[0,2],[1,2],[2,3],[1,2],[2,3],[0,2],[0,1],[1,3],[0,2],[1,2],[0,1],[2,3],[1,2],[1,2],[2,3],[0,2],[2,3],[0,2],[2,3],[0,2],[0,2],[2,3],[1,2],[2,3],[2,3],[2,3],[2,3],[2,3],[1,2],[1,2],[0,2],[0,1],[1,2],[0,2],[2,3],[1,2],[1,3],[1,2],[1,2],[2,3],[0,2],[0,2],[0,2],[1,2],[1,2],[0,1],[2,3],[0,2],[2,3],[0,2],[2,3],[0,2],[0,2],[0,3],[0,2],[2,3],[0,1],[1,2],[1,2],[1,2],[1,2],[1,2],[0,3],[1,2],[1,2],[0,3],[0,1],[2,3],[1,2],[1,2],[0,2],[0,2],[2,3],[1,2],[0,2],[1,2],[2,3],[0,2],[1,2],[0,1],[2,3],[0,1],[0,1],[0,2],[2,3],[1,2],[1,2],[2,3],[2,3],[2,3],[1,3],[1,2],[1,2],[2,3],[0,2],[0,1],[0,2],[2,3],[0,3],[1,2],[0,2],[0,2],[1,2],[0,2],[1,2],[1,2],[2,3],[2,3],[0,3],[0,2],[1,2],[0,2],[1,2],[2,3],[0,2],[2,3],[1,2],[1,2],[1,2],[0,2],[0,1],[0,2],[0,2],[0,2],[2,3],[0,2],[0,2],[0,2],[0,3],[0,3],[1,2],[1,2],[0,1],[1,2],[1,3],[0,3],[2,3],[0,2],[0,2],[1,3],[0,3],[1,2],[1,3],[2,3],[1,2],[0,2],[0,2],[1,3],[1,3],[0,2],[0,2],[1,3],[1,2],[1,2],[0,1],[1,2],[1,2],[1,2],[0,3],[0,1],[1,2],[0,2],[0,2],[1,2],[0,2],[0,2],[1,2],[0,2],[2,3],[1,2],[0,2],[1,3],[2,3],[2,3],[1,2],[1,2],[2,3],[2,3],[0,2],[2,3],[1,2],[1,2],[2,3],[0,2],[1,2],[0,2],[1,2],[1,2],[1,2],[0,2],[1,3],[1,3],[2,3],[1,2],[1,3],[2,3],[0,2],[0,2],[1,3],[0,2],[2,3],[0,2],[0,2],[1,2],[0,3],[0,2],[2,3],[1,2],[2,3],[0,1],[0,2],[1,2],[1,2],[1,2],[2,3],[1,2],[1,2],[2,3]],[[2,3],[2,3],[2,3],[1,3],[0,2],[2,3],[0,2],[2,3],[2,3],[0,2],[0,2],[2,3],[1,2],[1,2],[2,3],[0,3],[1,2],[1,2],[2,3],[2,3],[1,3],[0,2],[2,3],[1,2],[2,3],[0,2],[0,2],[0,2],[2,3],[1,2],[0,2],[0,2],[1,3],[2,3],[0,3],[2,3],[2,3],[1,2],[2,3],[0,2],[2,3],[0,2],[2,3],[1,3],[1,2],[1,2],[1,2],[1,2],[0,2],[0,2],[1,2],[1,3],[1,2],[1,2],[1,2],[1,2],[0,2],[1,2],[0,3],[1,3],[1,2],[1,2],[2,3],[2,3],[0,2],[0,2],[1,2],[2,3],[2,3],[0,2],[0,2],[1,2],[0,2],[2,3],[0,2],[2,3],[2,3],[1,2],[0,2],[0,3],[1,2],[2,3],[0,1],[0,2],[0,2],[2,3],[0,3],[0,3],[0,2],[0,1],[0,1],[1,2],[0,2],[0,2],[2,3],[1,3],[1,2],[0,3],[1,3],[0,3],[2,3],[1,2],[2,3],[0,2],[2,3],[1,3],[1,2],[1,2],[0,1],[1,2],[1,2],[2,3],[1,2],[1,2],[0,2],[1,2],[0,3],[0,2],[0,3],[0,2],[2,3],[1,2],[0,3],[0,2],[0,2],[1,2],[1,2],[2,3],[1,2],[0,1],[1,2],[0,2],[0,2],[0,2],[0,1],[1,2],[0,2],[0,3],[0,3],[2,3],[1,2],[1,2],[2,3],[2,3],[0,2],[1,2],[0,2],[0,2],[1,2],[1,2],[2,3],[1,2],[2,3],[2,3],[0,2],[2,3],[1,2],[0,1],[2,3],[0,2],[1,2],[0,2],[1,2],[1,2],[0,2],[2,3],[0,3],[1,2],[0,2],[1,2],[2,3],[2,3],[0,2],[0,2],[1,2],[0,2],[0,3],[0,2],[1,2],[0,1],[1,2],[2,3],[0,2],[2,3],[2,3],[0,2],[2,3],[0,2],[0,2],[1,2],[0,2],[2,3],[0,2],[2,3],[0,1],[0,2],[1,2],[1,3],[0,2],[1,2],[2,3],[1,2],[0,2],[2,3],[0,3],[2,3],[1,2],[0,2],[2,3],[1,3],[1,2],[2,3],[1,2],[0,1],[1,3],[2,3],[1,2],[2,3],[2,3],[0,1],[0,2],[1,2],[0,2],[1,2],[2,3],[0,3],[0,2],[0,2],[0,3],[0,1],[1,3],[1,2],[0,2],[1,3],[0,1],[2,3],[2,3],[0,3],[0,2],[0,1],[1,2],[1,3],[2,3],[1,2],[0,3],[2,3],[1,2],[2,3],[1,2],[1,2],[1,2],[1,2],[2,3],[2,3],[0,2],[2,3],[0,2],[0,2],[0,2],[0,2],[0,2],[1,2],[2,3],[1,2],[0,3],[1,2],[0,2],[2,3],[0,2],[1,2],[0,2],[1,2],[2,3],[0,2],[0,2],[0,2],[1,2],[2,3],[1,2],[2,3],[2,3],[2,3],[0,2],[1,2],[1,2],[1,2],[0,2],[2,3],[2,3],[2,3],[1,2],[1,3],[1,2],[0,2],[0,2],[2,3],[0,1],[2,3],[0,2],[1,2],[2,3],[1,2],[0,2],[1,2],[0,1],[0,1],[2,3],[0,2],[0,2],[2,3],[2,3],[1,2],[1,2],[0,2],[1,2],[1,2],[0,2],[1,2],[0,2],[0,2],[1,3],[0,2],[0,1],[0,1],[1,2],[2,3],[0,1],[1,2],[0,2],[0,1],[2,3],[2,3],[1,2],[1,3],[1,2],[2,3],[1,2],[1,2],[1,2],[1,2],[2,3],[1,2],[2,3],[2,3],[0,2],[1,2],[2,3],[0,2],[1,3],[2,3],[0,2],[1,2],[0,2],[2,3],[0,2],[2,3],[0,1],[2,3],[0,2],[2,3],[1,2],[2,3],[0,2],[0,1],[0,2],[0,2],[0,2],[1,2],[1,2],[0,3],[2,3],[1,2],[1,2],[1,3],[1,3],[0,2],[2,3],[0,1],[1,2],[0,1],[1,2],[0,2],[0,2],[1,2],[0,2],[0,2],[2,3],[0,2],[2,3],[2,3],[0,2],[2,3],[0,1],[2,3],[0,2],[2,3],[1,2],[2,3],[0,2],[0,2],[0,2],[2,3],[0,1],[0,3],[0,2],[2,3],[2,3],[1,2],[2,3],[1,2],[1,2],[0,1],[1,2],[0,2],[0,1],[0,2],[0,2],[2,3],[0,3],[0,2],[1,2],[1,2],[1,2],[0,2],[0,2],[2,3],[0,2],[0,2],[1,3],[1,3],[1,2],[2,3],[2,3],[0,2],[1,2],[0,3],[0,2],[1,2],[0,1],[2,3],[1,2],[0,3],[0,2],[0,3],[0,2],[1,2],[0,1],[2,3],[0,2],[1,2],[0,2],[1,3],[0,2],[0,3],[2,3],[1,2],[1,2],[1,2],[1,2],[0,2],[2,3],[2,3],[1,2],[0,2],[1,2],[1,2],[0,1],[0,2],[0,3],[1,2],[2,3],[0,1],[2,3],[0,2],[1,2],[1,2],[1,3],[2,3],[1,2],[0,2],[1,3],[0,2],[1,2],[0,2],[0,2],[1,3],[0,2],[2,3],[0,1],[0,3],[1,2],[1,2],[1,2],[1,2],[2,3],[0,2],[0,2],[0,2],[0,3],[2,3],[0,2],[0,2],[1,2],[2,3],[1,2],[2,3],[1,2],[0,1],[2,3],[0,1],[1,2],[2,3]]]
def setup_inputs(rng):
    return {"x": rng.standard_normal((N, 128, TOK), dtype=np.float32).astype(ml_dtypes.bfloat16), "w": rng.standard_normal((N, 128, 128), dtype=np.float32).astype(ml_dtypes.bfloat16)}
def reference(x, w):
    X, W = x.astype(np.float64), w.astype(np.float64)
    y = np.zeros((N, 128, TOK))
    for r in range(N):
        for t in range(TOK):
            for e in ROUTE[r][t]:
                y[r][:, t] += W[e].T @ X[r][:, t]
    return {"y": y.astype(ml_dtypes.bfloat16 if x.dtype != np.float64 else np.float64)}

@@ -1,0 +1,220 @@
+from concourse.bass import DstId, RemoteDMATransfer
+from concourse.mybir import AluOpType
+
+NCH = 2
+CW = 512 // NCH
+DL = 448
+DIST = 3
+DLEVELS = [[(0, 3, 1.0), (1, 3, 1.0)], [(0, 5, 0.0), (2, 5, 0.0)], [(3, 7, 1.0)]]
+
+SCRATCH = {
+    "xs": ("sbuf", [128, 512], "bfloat16"),
+    "w0": ("sbuf", [128, 128], "bfloat16"),
+    "w1": ("sbuf", [128, 128], "bfloat16"),
+    "w2": ("sbuf", [128, 128], "bfloat16"),
+    "w3": ("sbuf", [128, 128], "bfloat16"),
+    "wd": ("dram", [128, 128], "bfloat16"),
+    "dic": ("sbuf", [128, DL], "bfloat16"),
+    "xm0": ("sbuf", [128, 512], "bfloat16"),
+    "xm1": ("sbuf", [128, 512], "bfloat16"),
+    "xm2": ("sbuf", [128, 512], "bfloat16"),
+    "w2z": ("sbuf", [128, 128], "bfloat16"),
+    "nwz": ("sbuf", [128, 128], "bfloat16"),
+    "yo": ("sbuf", [128, 512], "bfloat16"),
+    "mk0": ("psum", [128, 512], "float32"),
+    "mk1": ("psum", [128, 512], "float32"),
+    "mk2": ("psum", [128, 512], "float32"),
+    "yp0": ("psum", [128, 512], "float32"),
+    "yp1": ("psum", [128, 512], "float32"),
+}
+SEMAPHORES = ["lx", "lw", "lwd", "a0", "a1", "a2", "a3", "rl", "snt", "dct", "pv", "pp",
+              "x0", "x1", "x2", "f2", "fn", "ym0", "ym1", "yc0", "yc1", "st0", "st1"]
+
+AL = "ABCDEFGHIJKLMNOPQRSTUVWXYZabcdefghijklmnopqrstuvwxyz0123456789+-"
+PAINT = {
+    (0, 1): "wbjJ3AAyTAQpwBqjM7JAPHwSXgd+43YiYrOyfq4AAh-DAolto4Rj-3AAl4BDZrZ6CJl-fAxfkNj+beAbQkrddhqrIwgpqleFfYUspqZbQgigecsYkMdolg7gZeVJoIjhlOqdSRgCchoSbVhMDfSZ6GRoWwImWQR23bTUorbSiEWZShRGUUuc",
+    (0, 2): "AAAIsAQdAhwPCYIVhKo+AiqwVpc70IIgsbYRk+5u4ny5JQoucSAm-zfalbBA4fyEB8dirSQhpGDWD19VwJyBkueTzrgmqRK1gejDCcfibKmaWXigdDxmfRo6gNWpvQNY0kmfTiK+cXo12dbYnueb4b4KpyBAMgJA",
+    (0, 3): "AATGAofEwsAhWA9YeV4f4b4rjqcZgAeB5o1Brr1A6b0wDBg67iQq77ASh3qPhphrSqe1wl5d1wVddeA3AekeUvTYVAoq+WCigi1LajlBXYjQxZXdOg9pmpCkOVUgonbPrlwgZmEUOjdAgreotPZeRvmQaPABpYZHxoRqFChU+SdZUDsyeap2",
+    (1, 0): "YLl7BoMb4lofGgJ4fDg-Ah7RqIqKIAhk16U8Mxoxhg-xKIp+kAyjoACJf1FAbOxQ53YSoDAgppmBehzNQslUQUjgyyAhYJ5CdasBnNoZH4osNEwePgHJmfJV4ib6NeXTMPgnQvLRhsDdVPZUsofcMrYspadppUBgChUSixiVdtuJcqq",
+    (1, 2): "4MZ8c4fCIAofwBLIa5guhY0bBsF3aTClNI+kZsXK0fZleVH7bi6L7o2LN7rANMnJDgLo4EPEdRAKmiYNYI+3AuYeJsYrgSVwNXKCmfbmCtibMO6joFPGca8P2dYtdGcZ4oshUnIYLlo44LhedmfYGA4MaDvoLj3PYLl9e",
+    (1, 3): "AAi5WAABA8AgL4LYi4AAJg24iojwQQSafA4FH-AwBoao8TdfoCzax3C6bv6pRePQ4poigHag6WA+MorSxfOR8vOarDEcRpECfp+FeMqwXgkOYABnntWndYo0uMZflBekVP+WRbNMaeor2NguarTfUe+bbnXuVSjKacZVXqdX4f2UTcW",
+    (2, 0): "AQAoaAAAAOAQCg-Ii38cAPpEmAn9AArO8aDJegBD7C-RrkeowsiT-PAfEwoz5i07llUdSspm8kMLcvqVOFoogVeVYhRgOR02GjhazcYgnAhXAEgiW6E-UeQ7TdP55WgYgdRrmkFRlkaH8YhgOfUVcmreRbnjKvKPolX2JWbSbIKfSYAnSWST",
+    (2, 1): "gf2Me4P8AA4k+43AhqorKe5pOsOmBIxa-UHxePo9vB0YA-MlgJZqgSAIiMJHKjyMRIiko4FB3Ak8O6lMYrhISZgZSRpqOBBhj3cd1H1Ixzachw7bbeeOhZxXAnY3bPaRVk+USEMPVXdZbaRbKSfRZC7aX9sbeSWlycX0VuhUg5XNVwe",
+    (2, 3): "AQAAaAAAwDQhXS3wKuKZhjWjB4e94uNOsoaol6Coge5ZBxoO49PaLoBomKAALb5rgVZoaQgexTEXJoBNnQmFVxgUzOthbCJTbVgJBqzmEYl4SfKfYgr5maNqnNoIidThtNRgV-NwmQZUhfU6CTbj43omTiy6cTfsZhUOkKfUnVnUQpE3XRFzhdS2QnbS6g",
+    (3, 0): "AAPQPIgsDWJfKICtNnNi4k3WDSh6NUAqywDxooCCLK7UEJcxBzwKxitAry3K8afnCyd57FZqe0EYjs6NggiTSCjkWg7Rq-ULZXI4GdPAAgmdGgJnugYKiY9MfVVvD9bQaG-MkuaAmQBl0bQxZVcZYu+aaveYnSstjZSQpLYU8L",
+    (3, 1): "AAAIOAQHAXYLlYvopqIkRh4YAyf4YPIfMY+OA1TWjWiwRImhDEIqqx0okQD25ifZ2xftNA5rWJBhd7kXrav+OYhrAIqciTAfZRFHfcUEAoriLSAejXZvUcsUggpLp9FoopgoxDafbUDgYiUyVKhTpa7dZpv4gXukQrR-ijaQlqLbQ6BeaRqI3RVMb",
+    (3, 2): "AQAIm4fCo-AAgAvAcooTAjSQAJqKQz4d+4Kpl5EBCgXlcvGrSB5kqFTEdXo8dI1wCgksJohj-o0QKuUIKhd4TMkdmACfmI3gpUS4ciiSDGA-qWAKwYe1ZVkZwNUjEGA40b2dYIv9F6GAmfbsdINY0NQNWLAgMc-eQMfGO",
+}
+
+
+def paint_ops(r, e):
+    f = PAINT[(r, e)]
+    ops = []
+    for i in range(0, len(f), 5):
+        u = sum(AL.index(f[i + k]) << (6 * k) for k in range(5))
+        ops.append((u >> 21, ((u >> 18) & 7) + 1, ((u >> 12) & 63) + 1, (u >> 3) & 511, (u & 7) + 1))
+    return ops
+
+
+def schedule(streams, dist):
+    sets = [[set(range(a, a + (n - 1) * s + 1, s)) for (a, s, n, sa, ss) in st] for st in streams]
+    preds, depth = {}, {}
+    for k, st in enumerate(sets):
+        for j in range(len(st)):
+            preds[(k, j)] = [(k, i) for i in range(j) if st[i] & st[j]]
+        for j in reversed(range(len(st))):
+            d = 0
+            for jj in range(j + 1, len(st)):
+                if st[j] & st[jj]:
+                    d = max(d, depth[(k, jj)] + 1)
+            depth[(k, j)] = d
+    done, order = {}, []
+    rem = sorted(preds)
+    t = 0
+    while rem:
+        ready = [o for o in rem if all(p in done for p in preds[o])]
+        o = max(ready, key=lambda o: (min([t - done[p] for p in preds[o]] + [dist]), depth[o], -o[0], -o[1]))
+        done[o] = t
+        order.append((o[0], streams[o[0]][o[1]], max([done[p] for p in preds[o]] + [-1])))
+        rem.remove(o)
+        t += 1
+    return order
+
+
+def did(topo, c):
+    rid, pid, _ = topo.addr(c)
+    return DstId(rid=rid, pnc=pid)
+
+
+def rank_program(g, core, T, topo):
+    S = T.sem
+    cores = list(T.cores)
+    relays = {}
+    for s in range(4):
+        c = cores[s]
+        off = [d for d in cores if topo.chip(d) != topo.chip(c)]
+        if not topo.may_write(c, off[0]):
+            base = topo.chip(c) * 8
+            for rc in (base + 2, base + 6):
+                dst = [d for d in off if topo.die(d) == topo.die(rc)][0]
+                relays[rc] = (s, dst)
+    rank = T.rank_of(core)
+    if rank is None:
+        if core in relays:
+            s, dst = relays[core]
+            rid, pid, _ = topo.addr(dst)
+            g.wait_ge(S.rl, 16)
+            g.remote_dma(T["w%d" % s][:], T.wd[:], S["a%d" % s], S.snt, pid, rid, 0x00FF)
+            g.wait_ge(S.snt, 8)
+        return
+
+    z = rank
+    wz = T["w%d" % z]
+    on = [d for d in cores if d != core and topo.chip(d) == topo.chip(core)]
+    off = [d for d in cores if topo.chip(d) != topo.chip(core)]
+    direct = topo.may_write(core, off[0])
+
+    g.scalar.dma_start(T.wd[:], T.w[:]).then_inc(S.lwd, 16)
+    g.scalar.dma_start(wz[:], T.w[:]).then_inc(S.lw, 16)
+    g.sync.dma_start(T.xs[:], T.x[:]).then_inc(S.lx, 16)
+
+    arr = S["a%d" % z]
+    g.wait_ge(S.lwd, 16)
+    if direct:
+        g.remote_dma_fused([
+            RemoteDMATransfer(dst_ids=[did(topo, d) for d in off], dma_engine_mask=0x00FF, remote_sem=arr,
+                              srcs=[T.wd[:]], dsts=[wz[:] for d in off]),
+            RemoteDMATransfer(dst_ids=[did(topo, d) for d in on], dma_engine_mask=0xFF00, remote_sem=arr,
+                              srcs=[T.wd[:]], dsts=[wz[:] for d in on]),
+        ], local_sem=S.snt)
+        g.wait_ge(S.snt, 16)
+    else:
+        mine = [rc for rc in relays if relays[rc][0] == z]
+        g.remote_dma_fused([
+            RemoteDMATransfer(dst_ids=[did(topo, d) for d in mine], dma_engine_mask=0xFFFF, remote_sem=S.rl,
+                              srcs=[T.wd[:]], dsts=[T.wd[:] for d in mine]),
+        ], local_sem=S.snt)
+        rid, pid, _ = topo.addr(on[0])
+        g.remote_dma(wz[:], T.wd[:], arr, S.snt, pid, rid, 0xFFFF)
+        g.wait_ge(S.snt, 32)
+
+    def count(s):
+        c = cores[s]
+        if topo.chip(c) == topo.chip(core):
+            return 8 if topo.may_write(c, off[0]) else 16
+        return 8
+    near = T.rank_of(on[0])
+    late = [T.rank_of(d) for d in off if not topo.may_write(d, core)][0]
+    mate = [T.rank_of(d) for d in off if topo.may_write(d, core)][0]
+    ex = [near, mate, late]
+    ops = [paint_ops(rank, e) for e in ex]
+    mk = [T.mk0, T.mk1, T.mk2]
+    xm = [T.xm0, T.xm1, T.xm2]
+    xsm = [S.x0, S.x1, S.x2]
+    yp = [T.yp0, T.yp1]
+    v = g.vector
+    pe = g.tensor
+
+    def paint(js, on_pe, sem):
+        order = schedule([ops[j] for j in js], DIST)
+        eng = pe if on_pe else v
+        synced = -1
+        for t, (k, (a, s, n, sa, ss), p) in enumerate(order):
+            if p > synced:
+                synced = max(p, t - DIST)
+                eng.wait_ge(sem, synced + 1)
+            dst = mk[js[k]][:, a:a + (n - 1) * s + 1:s]
+            if on_pe:
+                pe.matmul(dst, T.dic[0:1, 0:128], T.dic[0:1, sa:sa + (n - 1) * ss + 1:ss],
+                          start=True, stop=True).then_inc(sem, 1)
+            else:
+                v.tensor_copy(dst, T.dic[:, sa:sa + (n - 1) * ss + 1:ss]).then_inc(sem, 1)
+        return len(order)
+
+    v.memset(T.dic[:, 128:DL], 0.0).then_inc(S.dct, 1)
+    v.memset(T.dic[:, 0:128], 1.0).then_inc(S.dct, 1)
+    nd = 2
+    for lev in DLEVELS:
+        v.wait_ge(S.dct, nd)
+        for (st, step, val) in lev:
+            v.memset(T.dic[:, 256 + st:DL:step], val).then_inc(S.dct, 1)
+            nd += 1
+    v.wait_ge(S.dct, nd)
+    nv = paint([0], False, S.pv)
+    v.wait_ge(S.lw, 16)
+    v.tensor_tensor(T.w2z[:], wz[:], wz[:], AluOpType.add).then_inc(S.f2, 1)
+    v.tensor_tensor(T.nwz[:], T.dic[:, 128:256], wz[:], AluOpType.subtract).then_inc(S.fn, 1)
+    v.wait_ge(S.lx, 16)
+    v.wait_ge(S.pv, nv)
+    v.tensor_tensor(xm[0][:], T.xs[:], mk[0][:], AluOpType.mult).then_inc(xsm[0], 1)
+    v.wait_ge(S.pp, len(ops[1]) + len(ops[2]))
+    for j in (1, 2):
+        v.tensor_tensor(xm[j][:], T.xs[:], mk[j][:], AluOpType.mult).then_inc(xsm[j], 1)
+    for k in range(NCH):
+        v.wait_ge(S["ym%d" % k], 1)
+        v.tensor_copy(T.yo[:, k * CW:(k + 1) * CW], yp[k][:, 0:CW]).then_inc(S["yc%d" % k], 1)
+
+    pe.wait_ge(S.dct, nd)
+    paint([1, 2], True, S.pp)
+
+    def mm(lhsT, rhs, start, stop):
+        for k in range(NCH):
+            i = pe.matmul(yp[k][:, 0:CW], lhsT[:], rhs[:, k * CW:(k + 1) * CW], start=start, stop=stop)
+            if stop:
+                i.then_inc(S["ym%d" % k], 1)
+    pe.wait_ge(S.lx, 16)
+    pe.wait_ge(S.f2, 1)
+    mm(T.w2z, T.xs, True, False)
+    pe.wait_ge(S.fn, 1)
+    for j in range(3):
+        pe.wait_ge(xsm[j], 1)
+        mm(T.nwz, xm[j], False, False)
+    for j in range(3):
+        pe.wait_ge(S["a%d" % ex[j]], count(ex[j]))
+        mm(T["w%d" % ex[j]], xm[j], False, j == 2)
+
+    for k in range(NCH):
+        q = g.sync if k % 2 == 0 else g.scalar
+        q.wait_ge(S["yc%d" % k], 1)
+        q.dma_start(T.y[:, k * CW:(k + 1) * CW], T.yo[:, k * CW:(k + 1) * CW]).then_inc(S["st%d" % k], 16)
+        q.wait_ge(S["st%d" % k], 16)

@@ -4,7 +4,7 @@ from concourse.mybir import AluOpType
 NCH = 2
 CW = 512 // NCH
 DL = 448
-DIST = 3
+DIST = 6
 DLEVELS = [[(0, 3, 1.0), (1, 3, 1.0)], [(0, 5, 0.0), (2, 5, 0.0)], [(3, 7, 1.0)]]
 
 SCRATCH = {
@@ -32,23 +32,22 @@ SEMAPHORES = ["lx", "lw", "lwd", "a0", "a1", "a2", "a3", "rl", "snt", "dct", "pv
 
 AL = "ABCDEFGHIJKLMNOPQRSTUVWXYZabcdefghijklmnopqrstuvwxyz0123456789+-"
 PAINT = {
-    (0, 1): "wbjJ3AAyTAQpwBqjM7JAPHwSXgd+43YiYrOyfq4AAh-DAolto4Rj-3AAl4BDZrZ6CJl-fAxfkNj+beAbQkrddhqrIwgpqleFfYUspqZbQgigecsYkMdolg7gZeVJoIjhlOqdSRgCchoSbVhMDfSZ6GRoWwImWQR23bTUorbSiEWZShRGUUuc",
-    (0, 2): "AAAIsAQdAhwPCYIVhKo+AiqwVpc70IIgsbYRk+5u4ny5JQoucSAm-zfalbBA4fyEB8dirSQhpGDWD19VwJyBkueTzrgmqRK1gejDCcfibKmaWXigdDxmfRo6gNWpvQNY0kmfTiK+cXo12dbYnueb4b4KpyBAMgJA",
-    (0, 3): "AATGAofEwsAhWA9YeV4f4b4rjqcZgAeB5o1Brr1A6b0wDBg67iQq77ASh3qPhphrSqe1wl5d1wVddeA3AekeUvTYVAoq+WCigi1LajlBXYjQxZXdOg9pmpCkOVUgonbPrlwgZmEUOjdAgreotPZeRvmQaPABpYZHxoRqFChU+SdZUDsyeap2",
-    (1, 0): "YLl7BoMb4lofGgJ4fDg-Ah7RqIqKIAhk16U8Mxoxhg-xKIp+kAyjoACJf1FAbOxQ53YSoDAgppmBehzNQslUQUjgyyAhYJ5CdasBnNoZH4osNEwePgHJmfJV4ib6NeXTMPgnQvLRhsDdVPZUsofcMrYspadppUBgChUSixiVdtuJcqq",
-    (1, 2): "4MZ8c4fCIAofwBLIa5guhY0bBsF3aTClNI+kZsXK0fZleVH7bi6L7o2LN7rANMnJDgLo4EPEdRAKmiYNYI+3AuYeJsYrgSVwNXKCmfbmCtibMO6joFPGca8P2dYtdGcZ4oshUnIYLlo44LhedmfYGA4MaDvoLj3PYLl9e",
-    (1, 3): "AAi5WAABA8AgL4LYi4AAJg24iojwQQSafA4FH-AwBoao8TdfoCzax3C6bv6pRePQ4poigHag6WA+MorSxfOR8vOarDEcRpECfp+FeMqwXgkOYABnntWndYo0uMZflBekVP+WRbNMaeor2NguarTfUe+bbnXuVSjKacZVXqdX4f2UTcW",
-    (2, 0): "AQAoaAAAAOAQCg-Ii38cAPpEmAn9AArO8aDJegBD7C-RrkeowsiT-PAfEwoz5i07llUdSspm8kMLcvqVOFoogVeVYhRgOR02GjhazcYgnAhXAEgiW6E-UeQ7TdP55WgYgdRrmkFRlkaH8YhgOfUVcmreRbnjKvKPolX2JWbSbIKfSYAnSWST",
-    (2, 1): "gf2Me4P8AA4k+43AhqorKe5pOsOmBIxa-UHxePo9vB0YA-MlgJZqgSAIiMJHKjyMRIiko4FB3Ak8O6lMYrhISZgZSRpqOBBhj3cd1H1Ixzachw7bbeeOhZxXAnY3bPaRVk+USEMPVXdZbaRbKSfRZC7aX9sbeSWlycX0VuhUg5XNVwe",
-    (2, 3): "AQAAaAAAwDQhXS3wKuKZhjWjB4e94uNOsoaol6Coge5ZBxoO49PaLoBomKAALb5rgVZoaQgexTEXJoBNnQmFVxgUzOthbCJTbVgJBqzmEYl4SfKfYgr5maNqnNoIidThtNRgV-NwmQZUhfU6CTbj43omTiy6cTfsZhUOkKfUnVnUQpE3XRFzhdS2QnbS6g",
-    (3, 0): "AAPQPIgsDWJfKICtNnNi4k3WDSh6NUAqywDxooCCLK7UEJcxBzwKxitAry3K8afnCyd57FZqe0EYjs6NggiTSCjkWg7Rq-ULZXI4GdPAAgmdGgJnugYKiY9MfVVvD9bQaG-MkuaAmQBl0bQxZVcZYu+aaveYnSstjZSQpLYU8L",
-    (3, 1): "AAAIOAQHAXYLlYvopqIkRh4YAyf4YPIfMY+OA1TWjWiwRImhDEIqqx0okQD25ifZ2xftNA5rWJBhd7kXrav+OYhrAIqciTAfZRFHfcUEAoriLSAejXZvUcsUggpLp9FoopgoxDafbUDgYiUyVKhTpa7dZpv4gXukQrR-ijaQlqLbQ6BeaRqI3RVMb",
-    (3, 2): "AQAIm4fCo-AAgAvAcooTAjSQAJqKQz4d+4Kpl5EBCgXlcvGrSB5kqFTEdXo8dI1wCgksJohj-o0QKuUIKhd4TMkdmACfmI3gpUS4ciiSDGA-qWAKwYe1ZVkZwNUjEGA40b2dYIv9F6GAmfbsdINY0NQNWLAgMc-eQMfGO",
+    (0, 1): "AAAQRQmJAAAi3SAbebYRpjsgBHBroLLcS5L5dcADAndzAfSZ6GRoWwIDdRgSrbSiE AAo5gJgPIX9jOIVJiW4nokKBV4p5QZBo7BchnYphAnPZXTccIcApeae9XWkYIhajcqdSRg wLiArYceI8Qk0hvKgeYrPbMRrzexZvShqYyigT48jdd6ynOax1fZTMtgoRNrIPROw",
+    (0, 2): "AAAQAJk-gApocYR8B3CAgs-wIgmqRK1gejDmfTiK4KpyBAMgJA AP9wXYlQwZ2B9ofCfY5g5hcagNhP4hcgSAVafXDXmfQZW2dbYnueb4b AAAArAQoJrtHyQrai3ByqnqZ1shjY61fZ4rshdZtCiZDzmfPzrmfPJvmfRo6+cXo1",
+    (0, 3): "AQDYUwfuaD5saAATcTKApkmIPsOuqD9DxBI7YYjI+cNRMOaN4ADbrJEBpYZHxoRqF AACQlofEIVJb-IdgkzJeierBVrdUxl1Zb5VqiUQgQrcbcNYQZi7bOgobbdhW8iSIXKiRmV YgWi35jeKrBm3Sr7W3CrqgYYyAshzrXdOg9greotPZeRvdZUDsyeap2",
+    (1, 0): "AQGAUgd7IHQg3AACibjAMboTAZpmZLBoTCHdaa4OoeUvAQfORQYnhIC3XOgDwePgH Zg8IVYgjZdtcXBVorpSVwgZZVQjiom5qbSa7ePoWglR-X8N4hcfcXVYppUBgChUSi wPCQrwg444gs1JrIqvo5QhYQ6dB1BsRhdas8ZhwsNPeUsAnV55xiVdtmKbCr",
+    (1, 2): "AQAoEwsWISIneIA1K7hANgXaA+Aq5EEhi4JgNaTAVkPgS2dQwKAOT6CKkUgPmfXGA AAAwowgEIVAk4ohZjggdIg2YWZleKW0fW4XwNSBVueT8V2dOYe+cQ4ouCvYiueaIj ohFI-AA9Ar9C+Q3cWvKsalphrWTm7sigdwtKkbazkjcctgNUtr4MaDv",
+    (1, 3): "AQAwJYdpLAKmlBAredDGhh-QKxmMzOnYNTCuDlbCghipCvZS5ECfS+CgkOYAydUYLuVSjK AAA4iofMAVVYnYjJjySVJmVid4ORwoIjWlVPFmZVDdbLWxoUwZbdP5lacZVXqdX4f2UTcW AACI8okuAr8ZrQrVJ64wXcRgxBoao8wkmhyChNQ6xfOR82XPQ4pfbwsccRZrmdRI1",
+    (2, 0): "AgBwUAQBAAwkx4HCggAIFlMRI5kzQOsC8QAAnYAEbagJMcdWoPDeOFKwjPJDWbSbIKfSYA AAA4qQPGAVIgdoiJqsSVFNuAWafShWBlTIjfLfhcxfTdVnXPKVpgjYmTcPYnWiYQdnUTKb AAAA64gIArSh5Zr6fsQ63C1hsPKiA0podbxpsgKrNdRrr-UeQ7TdP55jaWTsPWQQv",
+    (2, 1): "AAAAAAQXKAAA9YAUJmIQVSuSAac0IJBkNATIms4BpqOBBmObiJIoYyGpeToLbaRbKSfRZC IJ45c4m6Rc1E2IVQhOYo4hYQj4niCdNdhrVRpmodKfNgmRlaBVQPSyWycX0VXNVwe BpuAzqW3A5eaOw9od+ArgrWwv9hRorqYlLthlkbrYrQJumYj4zofQo1uhUg5",
+    (2, 3): "AgBYBAQZAMjOo4PxeXoBmOtZComKAAahZFCZsVqMYssAGKbWTEokUaMCdOoQhfU6CnUQpE AQA4hAhxJVbdTgoRb0RVEhXAWJnfCVeNiJijfTqiVbR4lvcRZZYkPKbpeTRXaeQlZnbS6g Il8AvwZ9A4wp2CrvXZIrZifZr-cWRwFcYEsscTZzJrXw7tZOZttPW706bSo43XRFz",
+    (3, 0): "AQQ4SAP-wKrMz4DfYeDETfgJEzdQQF4rNITWbQiM3bOACNdSCMGdPAACdUbFydR6L AQA4WAQCoosC-BVRoQghNeMIVQhMBWwPOIp2OnJXljbaYAmRBl0bQxZsXUAebZXpizeSOa AgBQrIjFQ-5dn7rRh+Y3vLqxrKksQtAhoQ5phQi2fRXLrzfW4tImQDrIpQZ6JmS60YnSst",
+    (3, 1): "Ao2IOAh6IAvMe4QxjQIRYrpCC5rWJBYhrAIqciTAfZRFHfcUEALbQ6BeaRqI gPEIVAgH4poe8IiYgwaW5czBVFcdBZxcc9VvVYBkZhWeVvbTcaYiUyVKhTpa3RVMb AQAY2wPCQ-gf-42wk6guxdrAw4qtY4reQ573OYy2BhQo5mZPD1InbArXbYrrxeUTrBrU6vScPJw",
+    (3, 2): "wPCgUAA3AAAh1aAHHvgAKkSgBqiu6CmIpxEANcwHddb6JueS7LmfSDEueTIRQNWLA APIAV6jl4Z+HsYlvCqrV8eSIaQlbYWalblWIOPKVuePAm9A1oemfaAh AADArYgGI-Yp3grciNwseZcouyfRxuBjvJzomuxzCfmI3gpUS4wNSMrmfUUy",
 }
 
 
-def paint_ops(r, e):
-    f = PAINT[(r, e)]
+def decode(f):
     ops = []
     for i in range(0, len(f), 5):
         u = sum(AL.index(f[i + k]) << (6 * k) for k in range(5))
@@ -88,16 +87,19 @@ def did(topo, c):
 
 def rank_program(g, core, T, topo):
     S = T.sem
+    v = g.vector
+    pe = g.tensor
     cores = list(T.cores)
     relays = {}
     for s in range(4):
         c = cores[s]
+        base = topo.chip(c) * 8
         off = [d for d in cores if topo.chip(d) != topo.chip(c)]
         if not topo.may_write(c, off[0]):
-            base = topo.chip(c) * 8
             for rc in (base + 2, base + 6):
                 dst = [d for d in off if topo.die(d) == topo.die(rc)][0]
                 relays[rc] = (s, dst)
+
     rank = T.rank_of(core)
     if rank is None:
         if core in relays:
@@ -147,29 +149,40 @@ def rank_program(g, core, T, topo):
     late = [T.rank_of(d) for d in off if not topo.may_write(d, core)][0]
     mate = [T.rank_of(d) for d in off if topo.may_write(d, core)][0]
     ex = [near, mate, late]
-    ops = [paint_ops(rank, e) for e in ex]
     mk = [T.mk0, T.mk1, T.mk2]
     xm = [T.xm0, T.xm1, T.xm2]
     xsm = [S.x0, S.x1, S.x2]
     yp = [T.yp0, T.yp1]
-    v = g.vector
-    pe = g.tensor
 
     def paint(js, on_pe, sem):
-        order = schedule([ops[j] for j in js], DIST)
+        bufs, streams = [], []
+        for j in js:
+            for piece in PAINT[(rank, ex[j])].split(" "):
+                bufs.append(mk[j])
+                streams.append(decode(piece))
         eng = pe if on_pe else v
+        order = schedule(streams, DIST)
         synced = -1
         for t, (k, (a, s, n, sa, ss), p) in enumerate(order):
             if p > synced:
-                synced = max(p, t - DIST)
+                synced = p
                 eng.wait_ge(sem, synced + 1)
-            dst = mk[js[k]][:, a:a + (n - 1) * s + 1:s]
+            dst = bufs[k][:, a:a + (n - 1) * s + 1:s]
             if on_pe:
                 pe.matmul(dst, T.dic[0:1, 0:128], T.dic[0:1, sa:sa + (n - 1) * ss + 1:ss],
                           start=True, stop=True).then_inc(sem, 1)
             else:
                 v.tensor_copy(dst, T.dic[:, sa:sa + (n - 1) * ss + 1:ss]).then_inc(sem, 1)
         return len(order)
+
+    def mask_x(j):
+        v.tensor_tensor(xm[j][:], T.xs[:], mk[j][:], AluOpType.mult).then_inc(xsm[j], 1)
+
+    def mm(lhsT, rhs, start, stop):
+        for k in range(NCH):
+            i = pe.matmul(yp[k][:, 0:CW], lhsT[:], rhs[:, k * CW:(k + 1) * CW], start=start, stop=stop)
+            if stop:
+                i.then_inc(S["ym%d" % k], 1)
 
     v.memset(T.dic[:, 128:DL], 0.0).then_inc(S.dct, 1)
     v.memset(T.dic[:, 0:128], 1.0).then_inc(S.dct, 1)
@@ -186,32 +199,31 @@ def rank_program(g, core, T, topo):
     v.tensor_tensor(T.nwz[:], T.dic[:, 128:256], wz[:], AluOpType.subtract).then_inc(S.fn, 1)
     v.wait_ge(S.lx, 16)
     v.wait_ge(S.pv, nv)
-    v.tensor_tensor(xm[0][:], T.xs[:], mk[0][:], AluOpType.mult).then_inc(xsm[0], 1)
-    v.wait_ge(S.pp, len(ops[1]) + len(ops[2]))
-    for j in (1, 2):
-        v.tensor_tensor(xm[j][:], T.xs[:], mk[j][:], AluOpType.mult).then_inc(xsm[j], 1)
+    mask_x(0)
+
+    pe.wait_ge(S.dct, nd)
+    npp = paint([1, 2], True, S.pp)
+    v.wait_ge(S.pp, npp)
+    mask_x(1)
+    mask_x(2)
     for k in range(NCH):
         v.wait_ge(S["ym%d" % k], 1)
         v.tensor_copy(T.yo[:, k * CW:(k + 1) * CW], yp[k][:, 0:CW]).then_inc(S["yc%d" % k], 1)
 
-    pe.wait_ge(S.dct, nd)
-    paint([1, 2], True, S.pp)
-
-    def mm(lhsT, rhs, start, stop):
-        for k in range(NCH):
-            i = pe.matmul(yp[k][:, 0:CW], lhsT[:], rhs[:, k * CW:(k + 1) * CW], start=start, stop=stop)
-            if stop:
-                i.then_inc(S["ym%d" % k], 1)
     pe.wait_ge(S.lx, 16)
     pe.wait_ge(S.f2, 1)
     mm(T.w2z, T.xs, True, False)
     pe.wait_ge(S.fn, 1)
-    for j in range(3):
+    for j in (0, 1):
         pe.wait_ge(xsm[j], 1)
         mm(T.nwz, xm[j], False, False)
-    for j in range(3):
+    for j in (1, 0):
         pe.wait_ge(S["a%d" % ex[j]], count(ex[j]))
-        mm(T["w%d" % ex[j]], xm[j], False, j == 2)
+        mm(T["w%d" % ex[j]], xm[j], False, False)
+    pe.wait_ge(xsm[2], 1)
+    mm(T.nwz, xm[2], False, False)
+    pe.wait_ge(S["a%d" % late], count(late))
+    mm(T["w%d" % late], xm[2], False, True)
 
     for k in range(NCH):
         q = g.sync if k % 2 == 0 else g.scalar

from concourse.bass import DstId, RemoteDMATransfer
from concourse.mybir import AluOpType

NCH = 2
CW = 512 // NCH
DL = 448
DIST = 6
DLEVELS = [[(0, 3, 1.0), (1, 3, 1.0)], [(0, 5, 0.0), (2, 5, 0.0)], [(3, 7, 1.0)]]

SCRATCH = {
    "xs": ("sbuf", [128, 512], "bfloat16"),
    "w0": ("sbuf", [128, 128], "bfloat16"),
    "w1": ("sbuf", [128, 128], "bfloat16"),
    "w2": ("sbuf", [128, 128], "bfloat16"),
    "w3": ("sbuf", [128, 128], "bfloat16"),
    "wd": ("dram", [128, 128], "bfloat16"),
    "dic": ("sbuf", [128, DL], "bfloat16"),
    "xm0": ("sbuf", [128, 512], "bfloat16"),
    "xm1": ("sbuf", [128, 512], "bfloat16"),
    "xm2": ("sbuf", [128, 512], "bfloat16"),
    "w2z": ("sbuf", [128, 128], "bfloat16"),
    "nwz": ("sbuf", [128, 128], "bfloat16"),
    "yo": ("sbuf", [128, 512], "bfloat16"),
    "mk0": ("psum", [128, 512], "float32"),
    "mk1": ("psum", [128, 512], "float32"),
    "mk2": ("psum", [128, 512], "float32"),
    "yp0": ("psum", [128, 512], "float32"),
    "yp1": ("psum", [128, 512], "float32"),
}
SEMAPHORES = ["lx", "lw", "lwd", "a0", "a1", "a2", "a3", "rl", "snt", "dct", "pv", "pp",
              "x0", "x1", "x2", "f2", "fn", "ym0", "ym1", "yc0", "yc1", "st0", "st1"]

AL = "ABCDEFGHIJKLMNOPQRSTUVWXYZabcdefghijklmnopqrstuvwxyz0123456789+-"
PAINT = {
    (0, 1): "AAAQRQmJAAAi3SAbebYRpjsgBHBroLLcS5L5dcADAndzAfSZ6GRoWwIDdRgSrbSiE AAo5gJgPIX9jOIVJiW4nokKBV4p5QZBo7BchnYphAnPZXTccIcApeae9XWkYIhajcqdSRg wLiArYceI8Qk0hvKgeYrPbMRrzexZvShqYyigT48jdd6ynOax1fZTMtgoRNrIPROw",
    (0, 2): "AAAQAJk-gApocYR8B3CAgs-wIgmqRK1gejDmfTiK4KpyBAMgJA AP9wXYlQwZ2B9ofCfY5g5hcagNhP4hcgSAVafXDXmfQZW2dbYnueb4b AAAArAQoJrtHyQrai3ByqnqZ1shjY61fZ4rshdZtCiZDzmfPzrmfPJvmfRo6+cXo1",
    (0, 3): "AQDYUwfuaD5saAATcTKApkmIPsOuqD9DxBI7YYjI+cNRMOaN4ADbrJEBpYZHxoRqF AACQlofEIVJb-IdgkzJeierBVrdUxl1Zb5VqiUQgQrcbcNYQZi7bOgobbdhW8iSIXKiRmV YgWi35jeKrBm3Sr7W3CrqgYYyAshzrXdOg9greotPZeRvdZUDsyeap2",
    (1, 0): "AQGAUgd7IHQg3AACibjAMboTAZpmZLBoTCHdaa4OoeUvAQfORQYnhIC3XOgDwePgH Zg8IVYgjZdtcXBVorpSVwgZZVQjiom5qbSa7ePoWglR-X8N4hcfcXVYppUBgChUSi wPCQrwg444gs1JrIqvo5QhYQ6dB1BsRhdas8ZhwsNPeUsAnV55xiVdtmKbCr",
    (1, 2): "AQAoEwsWISIneIA1K7hANgXaA+Aq5EEhi4JgNaTAVkPgS2dQwKAOT6CKkUgPmfXGA AAAwowgEIVAk4ohZjggdIg2YWZleKW0fW4XwNSBVueT8V2dOYe+cQ4ouCvYiueaIj ohFI-AA9Ar9C+Q3cWvKsalphrWTm7sigdwtKkbazkjcctgNUtr4MaDv",
    (1, 3): "AQAwJYdpLAKmlBAredDGhh-QKxmMzOnYNTCuDlbCghipCvZS5ECfS+CgkOYAydUYLuVSjK AAA4iofMAVVYnYjJjySVJmVid4ORwoIjWlVPFmZVDdbLWxoUwZbdP5lacZVXqdX4f2UTcW AACI8okuAr8ZrQrVJ64wXcRgxBoao8wkmhyChNQ6xfOR82XPQ4pfbwsccRZrmdRI1",
    (2, 0): "AgBwUAQBAAwkx4HCggAIFlMRI5kzQOsC8QAAnYAEbagJMcdWoPDeOFKwjPJDWbSbIKfSYA AAA4qQPGAVIgdoiJqsSVFNuAWafShWBlTIjfLfhcxfTdVnXPKVpgjYmTcPYnWiYQdnUTKb AAAA64gIArSh5Zr6fsQ63C1hsPKiA0podbxpsgKrNdRrr-UeQ7TdP55jaWTsPWQQv",
    (2, 1): "AAAAAAQXKAAA9YAUJmIQVSuSAac0IJBkNATIms4BpqOBBmObiJIoYyGpeToLbaRbKSfRZC IJ45c4m6Rc1E2IVQhOYo4hYQj4niCdNdhrVRpmodKfNgmRlaBVQPSyWycX0VXNVwe BpuAzqW3A5eaOw9od+ArgrWwv9hRorqYlLthlkbrYrQJumYj4zofQo1uhUg5",
    (2, 3): "AgBYBAQZAMjOo4PxeXoBmOtZComKAAahZFCZsVqMYssAGKbWTEokUaMCdOoQhfU6CnUQpE AQA4hAhxJVbdTgoRb0RVEhXAWJnfCVeNiJijfTqiVbR4lvcRZZYkPKbpeTRXaeQlZnbS6g Il8AvwZ9A4wp2CrvXZIrZifZr-cWRwFcYEsscTZzJrXw7tZOZttPW706bSo43XRFz",
    (3, 0): "AQQ4SAP-wKrMz4DfYeDETfgJEzdQQF4rNITWbQiM3bOACNdSCMGdPAACdUbFydR6L AQA4WAQCoosC-BVRoQghNeMIVQhMBWwPOIp2OnJXljbaYAmRBl0bQxZsXUAebZXpizeSOa AgBQrIjFQ-5dn7rRh+Y3vLqxrKksQtAhoQ5phQi2fRXLrzfW4tImQDrIpQZ6JmS60YnSst",
    (3, 1): "Ao2IOAh6IAvMe4QxjQIRYrpCC5rWJBYhrAIqciTAfZRFHfcUEALbQ6BeaRqI gPEIVAgH4poe8IiYgwaW5czBVFcdBZxcc9VvVYBkZhWeVvbTcaYiUyVKhTpa3RVMb AQAY2wPCQ-gf-42wk6guxdrAw4qtY4reQ573OYy2BhQo5mZPD1InbArXbYrrxeUTrBrU6vScPJw",
    (3, 2): "wPCgUAA3AAAh1aAHHvgAKkSgBqiu6CmIpxEANcwHddb6JueS7LmfSDEueTIRQNWLA APIAV6jl4Z+HsYlvCqrV8eSIaQlbYWalblWIOPKVuePAm9A1oemfaAh AADArYgGI-Yp3grciNwseZcouyfRxuBjvJzomuxzCfmI3gpUS4wNSMrmfUUy",
}


def decode(f):
    ops = []
    for i in range(0, len(f), 5):
        u = sum(AL.index(f[i + k]) << (6 * k) for k in range(5))
        ops.append((u >> 21, ((u >> 18) & 7) + 1, ((u >> 12) & 63) + 1, (u >> 3) & 511, (u & 7) + 1))
    return ops


def schedule(streams, dist):
    sets = [[set(range(a, a + (n - 1) * s + 1, s)) for (a, s, n, sa, ss) in st] for st in streams]
    preds, depth = {}, {}
    for k, st in enumerate(sets):
        for j in range(len(st)):
            preds[(k, j)] = [(k, i) for i in range(j) if st[i] & st[j]]
        for j in reversed(range(len(st))):
            d = 0
            for jj in range(j + 1, len(st)):
                if st[j] & st[jj]:
                    d = max(d, depth[(k, jj)] + 1)
            depth[(k, j)] = d
    done, order = {}, []
    rem = sorted(preds)
    t = 0
    while rem:
        ready = [o for o in rem if all(p in done for p in preds[o])]
        o = max(ready, key=lambda o: (min([t - done[p] for p in preds[o]] + [dist]), depth[o], -o[0], -o[1]))
        done[o] = t
        order.append((o[0], streams[o[0]][o[1]], max([done[p] for p in preds[o]] + [-1])))
        rem.remove(o)
        t += 1
    return order


def did(topo, c):
    rid, pid, _ = topo.addr(c)
    return DstId(rid=rid, pnc=pid)


def rank_program(g, core, T, topo):
    S = T.sem
    v = g.vector
    pe = g.tensor
    cores = list(T.cores)
    relays = {}
    for s in range(4):
        c = cores[s]
        base = topo.chip(c) * 8
        off = [d for d in cores if topo.chip(d) != topo.chip(c)]
        if not topo.may_write(c, off[0]):
            for rc in (base + 2, base + 6):
                dst = [d for d in off if topo.die(d) == topo.die(rc)][0]
                relays[rc] = (s, dst)

    rank = T.rank_of(core)
    if rank is None:
        if core in relays:
            s, dst = relays[core]
            rid, pid, _ = topo.addr(dst)
            g.wait_ge(S.rl, 16)
            g.remote_dma(T["w%d" % s][:], T.wd[:], S["a%d" % s], S.snt, pid, rid, 0x00FF)
            g.wait_ge(S.snt, 8)
        return

    z = rank
    wz = T["w%d" % z]
    on = [d for d in cores if d != core and topo.chip(d) == topo.chip(core)]
    off = [d for d in cores if topo.chip(d) != topo.chip(core)]
    direct = topo.may_write(core, off[0])

    g.scalar.dma_start(T.wd[:], T.w[:]).then_inc(S.lwd, 16)
    g.scalar.dma_start(wz[:], T.w[:]).then_inc(S.lw, 16)
    g.sync.dma_start(T.xs[:], T.x[:]).then_inc(S.lx, 16)

    arr = S["a%d" % z]
    g.wait_ge(S.lwd, 16)
    if direct:
        g.remote_dma_fused([
            RemoteDMATransfer(dst_ids=[did(topo, d) for d in off], dma_engine_mask=0x00FF, remote_sem=arr,
                              srcs=[T.wd[:]], dsts=[wz[:] for d in off]),
            RemoteDMATransfer(dst_ids=[did(topo, d) for d in on], dma_engine_mask=0xFF00, remote_sem=arr,
                              srcs=[T.wd[:]], dsts=[wz[:] for d in on]),
        ], local_sem=S.snt)
        g.wait_ge(S.snt, 16)
    else:
        mine = [rc for rc in relays if relays[rc][0] == z]
        g.remote_dma_fused([
            RemoteDMATransfer(dst_ids=[did(topo, d) for d in mine], dma_engine_mask=0xFFFF, remote_sem=S.rl,
                              srcs=[T.wd[:]], dsts=[T.wd[:] for d in mine]),
        ], local_sem=S.snt)
        rid, pid, _ = topo.addr(on[0])
        g.remote_dma(wz[:], T.wd[:], arr, S.snt, pid, rid, 0xFFFF)
        g.wait_ge(S.snt, 32)

    def count(s):
        c = cores[s]
        if topo.chip(c) == topo.chip(core):
            return 8 if topo.may_write(c, off[0]) else 16
        return 8
    near = T.rank_of(on[0])
    late = [T.rank_of(d) for d in off if not topo.may_write(d, core)][0]
    mate = [T.rank_of(d) for d in off if topo.may_write(d, core)][0]
    ex = [near, mate, late]
    mk = [T.mk0, T.mk1, T.mk2]
    xm = [T.xm0, T.xm1, T.xm2]
    xsm = [S.x0, S.x1, S.x2]
    yp = [T.yp0, T.yp1]

    def paint(js, on_pe, sem):
        bufs, streams = [], []
        for j in js:
            for piece in PAINT[(rank, ex[j])].split(" "):
                bufs.append(mk[j])
                streams.append(decode(piece))
        eng = pe if on_pe else v
        order = schedule(streams, DIST)
        synced = -1
        for t, (k, (a, s, n, sa, ss), p) in enumerate(order):
            if p > synced:
                synced = p
                eng.wait_ge(sem, synced + 1)
            dst = bufs[k][:, a:a + (n - 1) * s + 1:s]
            if on_pe:
                pe.matmul(dst, T.dic[0:1, 0:128], T.dic[0:1, sa:sa + (n - 1) * ss + 1:ss],
                          start=True, stop=True).then_inc(sem, 1)
            else:
                v.tensor_copy(dst, T.dic[:, sa:sa + (n - 1) * ss + 1:ss]).then_inc(sem, 1)
        return len(order)

    def mask_x(j):
        v.tensor_tensor(xm[j][:], T.xs[:], mk[j][:], AluOpType.mult).then_inc(xsm[j], 1)

    def mm(lhsT, rhs, start, stop):
        for k in range(NCH):
            i = pe.matmul(yp[k][:, 0:CW], lhsT[:], rhs[:, k * CW:(k + 1) * CW], start=start, stop=stop)
            if stop:
                i.then_inc(S["ym%d" % k], 1)

    v.memset(T.dic[:, 128:DL], 0.0).then_inc(S.dct, 1)
    v.memset(T.dic[:, 0:128], 1.0).then_inc(S.dct, 1)
    nd = 2
    for lev in DLEVELS:
        v.wait_ge(S.dct, nd)
        for (st, step, val) in lev:
            v.memset(T.dic[:, 256 + st:DL:step], val).then_inc(S.dct, 1)
            nd += 1
    v.wait_ge(S.dct, nd)
    nv = paint([0], False, S.pv)
    v.wait_ge(S.lw, 16)
    v.tensor_tensor(T.w2z[:], wz[:], wz[:], AluOpType.add).then_inc(S.f2, 1)
    v.tensor_tensor(T.nwz[:], T.dic[:, 128:256], wz[:], AluOpType.subtract).then_inc(S.fn, 1)
    v.wait_ge(S.lx, 16)
    v.wait_ge(S.pv, nv)
    mask_x(0)

    pe.wait_ge(S.dct, nd)
    npp = paint([1, 2], True, S.pp)
    v.wait_ge(S.pp, npp)
    mask_x(1)
    mask_x(2)
    for k in range(NCH):
        v.wait_ge(S["ym%d" % k], 1)
        v.tensor_copy(T.yo[:, k * CW:(k + 1) * CW], yp[k][:, 0:CW]).then_inc(S["yc%d" % k], 1)

    pe.wait_ge(S.lx, 16)
    pe.wait_ge(S.f2, 1)
    mm(T.w2z, T.xs, True, False)
    pe.wait_ge(S.fn, 1)
    for j in (0, 1):
        pe.wait_ge(xsm[j], 1)
        mm(T.nwz, xm[j], False, False)
    for j in (1, 0):
        pe.wait_ge(S["a%d" % ex[j]], count(ex[j]))
        mm(T["w%d" % ex[j]], xm[j], False, False)
    pe.wait_ge(xsm[2], 1)
    mm(T.nwz, xm[2], False, False)
    pe.wait_ge(S["a%d" % late], count(late))
    mm(T["w%d" % late], xm[2], False, True)

    for k in range(NCH):
        q = g.sync if k % 2 == 0 else g.scalar
        q.wait_ge(S["yc%d" % k], 1)
        q.dma_start(T.y[:, k * CW:(k + 1) * CW], T.yo[:, k * CW:(k + 1) * CW]).then_inc(S["st%d" % k], 16)
        q.wait_ge(S["st%d" % k], 16)
